import numpy as np
import ml_dtypes


def mxq(x, axis, fmt="e4m3"):
    dtype, down = {"e4m3": (ml_dtypes.float8_e4m3fn, 7), "e5m2": (ml_dtypes.float8_e5m2, 14)}[fmt]
    v = np.moveaxis(np.asarray(x, np.float32).astype(ml_dtypes.bfloat16).astype(np.float64), axis, -1)
    blocks = v.reshape(v.shape[:-1] + (-1, 32))
    amax = np.abs(blocks).max(-1, keepdims=True)
    byte = np.maximum(np.where(amax > 0, np.frexp(amax)[1] - 1 + 127, 0) - down, 1)
    scale = np.exp2(byte - 127.0)
    codes = (blocks / scale).astype(np.float32).astype(dtype).astype(np.float64)
    return np.moveaxis((codes * scale).reshape(v.shape), -1, axis)


WIDE = False


def mx_kscale(k):
    if not WIDE:
        return np.ones(k)
    levels = np.array([10, -10, 5, -5, 0])
    if k % 512:
        return np.exp2(np.random.permutation(np.resize(levels, k // 32))).repeat(32)
    a = np.empty((k // 512, 16))
    for p in range(k // 512):
        a[p, :8] = np.random.permutation(np.resize(levels, 8))
        for g in range(8):
            far = levels[np.abs(levels - a[p, g]) >= 10]
            a[p, g + 8] = far[np.random.randint(len(far))]
    return np.exp2(a.ravel()).repeat(32)


def f64(x):
    return np.asarray(x).astype(np.float64)


def striped(idx):
    return np.tile(idx.reshape(-1, 16).T, (8, 1)).astype(np.uint16)


def unstriped(offs):
    return offs[:16].T.reshape(-1).astype(np.int64)


E2M1 = np.array([0.0, 0.5, 1.0, 1.5, 2.0, 3.0, 4.0, 6.0, -0.0, -0.5, -1.0, -1.5, -2.0, -3.0, -4.0, -6.0])


def pack_weight(w, fmt):
    k, n = w.shape
    w = f64(np.asarray(w, np.float32).astype(ml_dtypes.bfloat16)).reshape(k // 32, 32, n)
    amax = np.abs(w).max(1)
    if fmt == "e4m3":
        byte = np.frexp(amax)[1] - 1 + 127 - 7
    else:
        mant, ex = np.frexp(amax / 6.0)
        byte = np.where(mant > 0.5, ex, ex - 1) + 127
    byte = np.clip(np.where(amax > 0, byte, 1), 1, 254)
    scaled = (w * np.exp2(127.0 - byte)[:, None, :]).reshape(k, n).astype(np.float32)
    by_word = np.ascontiguousarray(scaled.reshape(k // 512, 128, 4, n).transpose(0, 1, 3, 2))
    if fmt == "e4m3":
        words = by_word.astype(ml_dtypes.float8_e4m3fn).view(np.uint8)
    else:
        c = by_word.astype(ml_dtypes.float4_e2m1fn).view(np.uint8) & 0xF
        words = (c[..., 0::2] | (c[..., 1::2] << 4)).reshape(k // 512, 128, 2 * n)
    return np.ascontiguousarray(words), np.ascontiguousarray(byte.astype(np.uint8).reshape(k // 512, 16, n))


def unpack_weight(words, scales, fmt):
    g, _, n = scales.shape
    words = np.ascontiguousarray(words).reshape(g, 128, n, -1)
    if fmt == "e4m3":
        vals = words.view(ml_dtypes.float8_e4m3fn).astype(np.float64)
    else:
        nib = np.empty((g, 128, n, 4), np.uint8)
        nib[..., 0::2] = words & 0xF
        nib[..., 1::2] = words >> 4
        vals = E2M1[nib]
    vals = vals * np.repeat(np.exp2(scales.astype(np.float64) - 127.0), 8, axis=1)[..., None]
    return vals.transpose(0, 1, 3, 2).reshape(g * 512, n)


def gelu(v):
    return 0.5 * v * (1.0 + np.tanh(np.sqrt(2.0 / np.pi) * (v + 0.044715 * v**3)))


K, T, S, H, T2, P, N = 1024, 4096, 1024, 512, 2048, 1024, 384

def setup_inputs():
    n = np.random.standard_normal
    s = mx_kscale(K)[:, None]
    u = mx_kscale(H)[:, None]
    d = {}
    d["tab_words"], d["tab_scales"] = pack_weight(n((K, T)) * s, "e4m3")
    d["offs"] = striped(np.random.permutation(T)[:S])
    d["offs2"] = striped(np.random.permutation(T2)[:S])
    d["offs3"] = striped(np.random.permutation(T2)[:P])
    d["offs4"] = striped(np.random.permutation(T2)[:P])
    d["w1"] = (n((K, H)) * 1.5 / K**0.5 / s).astype(np.float32)
    d["w2_words"], d["w2_scales"] = pack_weight(n((K, H)) * 1.5 / K**0.5 / s * u.T, "e2m1")
    d["w3_words"], d["w3_scales"] = pack_weight(n((K, H)) * 1.5 / K**0.5 / s * u.T, "e4m3")
    d["wgs"] = np.exp(0.3 * n((128, S))).astype(np.float32)
    d["page0"] = (n((H, T2)) * u).astype(np.float32)
    d["gain"] = np.exp(0.4 * n(H)).astype(np.float32)
    d["w4"] = (n((H, N)) * 0.9 / H**0.5 / u).astype(np.float32)
    d["wgo"] = np.exp(0.3 * n((128, P))).astype(np.float32)
    d["page1"] = n((N, T2)).astype(np.float32)
    return d

def reference(tab_words, tab_scales, offs, offs2, offs3, offs4, w1, w2_words, w2_scales, w3_words, w3_scales, wgs, page0, gain, w4, wgo, page1):
    v = unpack_weight(tab_words, tab_scales, "e4m3")[:, unstriped(offs)]
    d1 = np.tanh(mxq(f64(w1), 0, "e4m3").T @ v)
    d2 = unpack_weight(w2_words, w2_scales, "e2m1").T @ v
    d3 = unpack_weight(w3_words, w3_scales, "e4m3").T @ v
    h = np.maximum(d1 * d2, d1 * d3)
    page = f64(page0).copy()
    page[:, unstriped(offs2)] = np.tile(f64(wgs), (H // 128, 1)) * h
    x = f64(gain)[:, None] * page[:, unstriped(offs3)]
    e = mxq(f64(w4), 0, "e4m3").T @ mxq(x, 0, "e4m3")
    y = np.exp(-np.square(e))
    out = f64(page1).copy()
    out[:, unstriped(offs4)] = np.tile(f64(wgo), (N // 128, 1)) * y
    return out

@@ -1,0 +1,276 @@
+from contextlib import ExitStack
+
+import concourse.mybir as mybir
+from concourse.masks import make_identity
+
+K, T, S, H, T2, PL, N = 1024, 4096, 1024, 512, 2048, 1024, 384
+FLOPS = 3 * 2 * K * H * S + 2 * H * N * PL
+
+F32 = mybir.dt.float32
+BF16 = mybir.dt.bfloat16
+I32 = mybir.dt.int32
+U32 = mybir.dt.uint32
+U16 = mybir.dt.uint16
+U8 = mybir.dt.uint8
+FP8X4 = mybir.dt.float8_e4m3fn_x4
+FP4X4 = mybir.dt.float4_e2m1fn_x4
+ACT = mybir.ActivationFunctionType
+ALU = mybir.AluOpType
+
+P = 128
+PASSES = K // 512
+ROW_TILES = H // P
+OUT_TILES = N // P
+HALF = 512
+UNIT = 256
+
+
+def cols16(lo, hi):
+    return slice(lo // 16, hi // 16)
+
+
+def tile_list_module_discharge_page_kernel(
+    tc, tab_words, tab_scales, offs, offs2, offs3, offs4, w1, w2_words, w2_scales,
+    w3_words, w3_scales, wgs, page0, gain, w4, wgo, page1, out,
+):
+    nc = tc.nc
+    with ExitStack() as ctx:
+        keep = ctx.enter_context(tc.tile_pool(name="keep", bufs=1))
+        ring = ctx.enter_context(tc.tile_pool(name="ring", bufs=2))
+        psum = ctx.enter_context(tc.psum_pool(name="psum", bufs=1))
+
+        def bank(b, shape, dtype):
+            return psum.tile(shape, dtype, name="bank%d" % b, tag="bank%d" % b)
+
+        tab = [keep.tile([P, T], U32, name="tab%d" % a, tag="tab%d" % a, align_bytes=64) for a in range(PASSES)]
+        tab_sc = keep.tile([P, T], U8, align_bytes=64)
+        w_sc = keep.tile([P, PASSES, H], U8, align_bytes=64)
+        v_sc0 = keep.tile([P, S], U8, align_bytes=64)
+        v_sc1 = keep.tile([P, S], U8, align_bytes=64)
+        v = [keep.tile([P, S], U32, name="v%d" % a, align_bytes=64) for a in range(PASSES)]
+        list1 = keep.tile([P, S // 16], U16)
+        list2 = keep.tile([P, S // 16], U16)
+        list3 = keep.tile([P, PL // 16], U16)
+        list4 = keep.tile([P, PL // 16], U16)
+        w1_first = [keep.tile([P, 4, P], F32, name="w1f%d" % a, tag="w1f%d" % a) for a in range(PASSES)]
+        w1_rest = [keep.tile([P, 4, H - P], F32, name="w1r%d" % a) for a in range(PASSES)]
+        w2_sb = keep.tile([P, PASSES, 2 * H], U8, align_bytes=64)
+        w3_first = keep.tile([P, PASSES, P], U32, align_bytes=64)
+        w3_rest = keep.tile([P, PASSES, H - P], U32, align_bytes=64)
+        wgs_sb = keep.tile([P, S], F32)
+        wgo_sb = keep.tile([P, PL], F32)
+        page = [keep.tile([P, T2], F32, name="page%d" % t, align_bytes=64) for t in range(ROW_TILES)]
+        res = [keep.tile([P, T2], F32, name="res%d" % n, align_bytes=64) for n in range(OUT_TILES)]
+        w4_raw = keep.tile([P, 4, N], F32)
+        gain_sb = keep.tile([P, ROW_TILES], F32)
+        warm = keep.tile([P, 8], F32)
+        warm2 = keep.tile([P, 8], F32)
+
+        nc.vector.memset(tab_sc[:].bitcast(I32), 0)
+        nc.vector.memset(v_sc1[:].bitcast(I32), 0)
+        nc.vector.memset(w_sc[:].rearrange("p a c -> p (a c)").bitcast(I32), 0)
+        nc.vector.memset(warm[:], 0.0)
+        nc.scalar.activation(out=warm2[:], in_=warm[:], func=ACT.Exp)
+
+        def load_tab(a, lo, hi):
+            nc.sync.dma_start(out=tab[a][:, lo:hi].bitcast(I32),
+                              in_=tab_words[a, :, lo:hi, :].rearrange("p t i -> p (t i)").bitcast(I32))
+
+        def load_weight_scales(src, row, q):
+            nc.sync.dma_start(out=w_sc[32 * q + row:32 * q + row + 4].bitcast(I32),
+                              in_=src[:, 4 * q:4 * q + 4, :].rearrange("a r c -> r a c").bitcast(I32))
+
+        w1_k = w1.rearrange("(a p j) c -> a p j c", a=PASSES, j=4)
+        w3_w = w3_words.rearrange("a p c i -> p a (c i)")
+
+        load_tab(0, 0, T)
+        for q in range(4):
+            nc.sync.dma_start(out=tab_sc[32 * q:32 * q + 8, :].bitcast(I32),
+                              in_=tab_scales[:, 4 * q:4 * q + 4, :].bitcast(I32))
+        nc.sync.dma_start(list1[:], offs)
+        nc.sync.dma_start(out=w1_first[0][:], in_=w1_k[0][:, :, 0:P])
+        load_tab(1, 0, T // 2)
+        nc.sync.dma_start(out=w1_first[1][:], in_=w1_k[1][:, :, 0:P])
+        nc.vector.tensor_copy(v_sc0[:], tab_sc[:].indirect(list1[:]))
+        for q in range(4):
+            nc.sync.dma_start(out=v_sc1[32 * q:32 * q + 4, :].bitcast(I32),
+                              in_=v_sc0[32 * q + 4:32 * q + 8, :].bitcast(I32))
+        for q in range(2):
+            load_weight_scales(w2_scales, 0, q)
+        load_tab(1, T // 2, T)
+        nc.sync.dma_start(out=w2_sb[:].bitcast(I32), in_=w2_words.rearrange("a p c -> p a c").bitcast(I32))
+        for q in range(2, 4):
+            load_weight_scales(w2_scales, 0, q)
+        for q in range(4):
+            load_weight_scales(w3_scales, 4, q)
+        nc.sync.dma_start(out=w3_first[:].bitcast(I32), in_=w3_w[:, :, 0:4 * P].bitcast(I32))
+        nc.sync.dma_start(out=wgs_sb[:], in_=wgs)
+        nc.sync.dma_start(list2[:], offs2)
+        nc.sync.dma_start(out=page[0][:], in_=page0[0:P, :])
+        for a in range(PASSES):
+            nc.sync.dma_start(out=w1_rest[a][:], in_=w1_k[a][:, :, P:H])
+        nc.sync.dma_start(out=w3_rest[:].bitcast(I32), in_=w3_w[:, :, 4 * P:4 * H].bitcast(I32))
+        nc.sync.dma_start(list3[:], offs3)
+        with nc.allow_non_contiguous_dma(reason="one gain a partition"):
+            nc.sync.dma_start(out=gain_sb[:], in_=gain.rearrange("(t p) -> p t", p=P))
+        nc.sync.dma_start(out=w4_raw[:], in_=w4.rearrange("(p j) n -> p j n", j=4))
+        for t in range(1, ROW_TILES):
+            nc.sync.dma_start(out=page[t][:], in_=page0[t * P:(t + 1) * P, :])
+        nc.sync.dma_start(list4[:], offs4)
+        nc.sync.dma_start(out=wgo_sb[:], in_=wgo)
+        for n in range(OUT_TILES):
+            nc.sync.dma_start(out=res[n][:], in_=page1[n * P:(n + 1) * P, :])
+
+        v_sc = [v_sc0, v_sc1]
+        nc.vector.tensor_copy(v[0][:], tab[0][:].indirect(list1[:]))
+
+        def interleave(dst, src):
+            nc.scalar.copy(out=dst.rearrange("p (c i) j -> p c j i", i=4),
+                           in_=src.rearrange("p j (c i) -> p c j i", i=4))
+
+        def quantise_w1(t):
+            grouped = ring.tile([P, PASSES, P, 4], BF16, name="w1g", align_bytes=64)
+            for a in range(PASSES):
+                src = w1_first[a][:] if t == 0 else w1_rest[a][:, :, (t - 1) * P:t * P]
+                interleave(grouped[:, a], src)
+            codes = keep.tile([P, PASSES * P], U32, name="w1q%d" % t, align_bytes=64)
+            scales = keep.tile([P, PASSES * P], U8, name="w1s%d" % t, align_bytes=64)
+            nc.vector.quantize_mx(out=codes[:].bitcast(FP8X4), scales=scales[:],
+                                  in_=grouped[:].rearrange("p a c j -> p (a c j)"))
+            return codes, scales
+
+        w1q = [quantise_w1(0)]
+        for c in range(S // HALF):
+            nc.vector.tensor_copy(v[1][:, c * HALF:(c + 1) * HALF],
+                                  tab[1][:].indirect(list1[:, cols16(c * HALF, (c + 1) * HALF)]))
+        ident_f = keep.tile([P, P], F32, tag="tab1", align_bytes=64)
+        ident_bf = keep.tile([P, P], BF16, tag="tab0", align_bytes=64)
+        make_identity(nc, ident_f[:])
+        nc.scalar.copy(out=ident_bf[:], in_=ident_f[:])
+
+        def products(t):
+            rows = slice(t * P, (t + 1) * P)
+            p2 = keep.tile([P, S], F32, name="p2")
+            p3 = keep.tile([P, S], F32, name="p3")
+            codes, scales = w1q[t]
+            for c in range(S // HALF):
+                cs = slice(c * HALF, (c + 1) * HALF)
+                acc = [bank(3 * c + i, [P, HALF], F32) for i in range(3)]
+                for i in range(3):
+                    for a in range(PASSES):
+                        if i == 0:
+                            w = codes[:, a * P:(a + 1) * P].bitcast(FP8X4)
+                            ws = scales[:, a * P:(a + 1) * P]
+                        elif i == 1:
+                            w = w2_sb[:, a, 2 * t * P:2 * (t + 1) * P].bitcast(FP4X4)
+                            ws = w_sc[:, a, rows]
+                        else:
+                            src = w3_first[:, a, :] if t == 0 else w3_rest[:, a, (t - 1) * P:t * P]
+                            w = src.bitcast(FP8X4)
+                            ws = w_sc[4:P, a, rows]
+                        nc.tensor.matmul_mx(out=acc[i][:], lhsT=w, lhsT_scale=ws,
+                                            rhs=v[a][:, cs].bitcast(FP8X4), rhs_scale=v_sc[a][:, cs],
+                                            start=(a == 0), stop=(a == PASSES - 1))
+                d1 = ring.tile([P, HALF], F32, name="d1")
+                nc.scalar.activation(out=d1[:], in_=acc[0][:], func=ACT.Tanh)
+                nc.vector.tensor_tensor(p2[:, cs], acc[1][:], d1[:], ALU.mult)
+                nc.vector.tensor_tensor(p3[:, cs], acc[2][:], d1[:], ALU.mult)
+            return p2, p3
+
+        x_bf = keep.tile([P, ROW_TILES, PL], BF16, align_bytes=64)
+
+        def pick(t, lo, hi, dense):
+            nc.vector.tensor_copy(dense, page[t][:].indirect(list3[:, cols16(lo, hi)]))
+
+        def apply_gain(t, lo, hi, dense):
+            nc.scalar.activation(out=x_bf[:, t, lo:hi], in_=dense, func=ACT.Copy, scale=gain_sb[:, t:t + 1])
+
+        w4q = keep.tile([P, N], U32, align_bytes=64)
+        w4s = keep.tile([P, N], U8, align_bytes=64)
+
+        def quantise_w4():
+            grouped = keep.tile([P, N, 4], BF16, name="w4g", align_bytes=64)
+            interleave(grouped[:], w4_raw[:])
+            for lo, hi in ((0, 256), (256, N)):
+                nc.vector.quantize_mx(out=w4q[:, lo:hi].bitcast(FP8X4), scales=w4s[:, lo:hi],
+                                      in_=grouped[:, lo:hi, :].rearrange("p c j -> p (c j)"))
+
+        ps = products(0)
+        for t in range(ROW_TILES):
+            h = keep.tile([P, S], F32, name="h", tag="h")
+            nc.vector.tensor_tensor(h[:], ps[0][:], ps[1][:], ALU.max)
+            if t + 1 < ROW_TILES:
+                w1q.append(quantise_w1(t + 1))
+                ps = products(t + 1)
+            if t == 1:
+                quantise_w4()
+            nc.vector.tensor_tensor(page[t][:].indirect(list2[:]), h[:], wgs_sb[:], ALU.mult)
+            first = ring.tile([P, UNIT], F32, name="first")
+            pick(t, 0, UNIT, first[:])
+            apply_gain(t, 0, UNIT, first[:])
+
+        late = keep.tile([P, ROW_TILES * UNIT + 2 * HALF], F32, name="late", tag="h")
+        second = [(t, UNIT, HALF, late[:, t * UNIT:(t + 1) * UNIT]) for t in range(ROW_TILES)]
+        upper = [(t, HALF, PL, late[:, ROW_TILES * UNIT + t * HALF:ROW_TILES * UNIT + (t + 1) * HALF])
+                 for t in range(2)]
+        for job in second + upper:
+            pick(*job)
+
+        xq = keep.tile([P, PL], U32, align_bytes=64)
+        xs = keep.tile([P, PL], U8, align_bytes=64)
+        y = [keep.tile([P, PL], F32, name="y%d" % n) for n in range(OUT_TILES)]
+
+        def regroup(u):
+            us = slice(u * UNIT, (u + 1) * UNIT)
+            turned = bank(6, [P, 2, H], BF16)
+            for b in range(2):
+                lo = u * UNIT + b * P
+                for t in range(ROW_TILES):
+                    nc.tensor.transpose(turned[:, b, t * P:(t + 1) * P], x_bf[:, t, lo:lo + P], ident_bf[:])
+            pairs = ring.tile([P, 2, 2, P], F32, name="pairs")
+            nc.scalar.copy(out=pairs[:], in_=turned[:].bitcast(F32).rearrange("p b (m e) -> p b e m", e=2))
+            back = bank(7, [P, 2, 2, P], F32)
+            for b in range(2):
+                for e in range(2):
+                    nc.tensor.transpose(back[:, b, e, :], pairs[:, b, e, :], ident_f[:])
+            words = keep.tile([P, 2, P, 2], F32, name="words%d" % u, tag="words%d" % u, align_bytes=64)
+            nc.scalar.copy(out=words[:], in_=back[:].rearrange("p b e c -> p b c e"))
+            nc.vector.quantize_mx(out=xq[:, us].bitcast(FP8X4), scales=xs[:, us],
+                                  in_=words[:].rearrange("p b c e -> p (b c e)").bitcast(BF16))
+
+        def features(u):
+            us = slice(u * UNIT, (u + 1) * UNIT)
+            for n in range(OUT_TILES):
+                e_acc = bank(3 * (u % 2) + n, [P, UNIT], F32)
+                nc.tensor.matmul_mx(out=e_acc[:], lhsT=w4q[:, n * P:(n + 1) * P].bitcast(FP8X4),
+                                    lhsT_scale=w4s[:, n * P:(n + 1) * P],
+                                    rhs=xq[:, us].bitcast(FP8X4), rhs_scale=xs[:, us], start=True, stop=True)
+                sq = ring.tile([P, UNIT], F32, name="sq")
+                nc.scalar.activation(out=sq[:], in_=e_acc[:], func=ACT.Square)
+                nc.scalar.activation(out=y[n][:, us], in_=sq[:], func=ACT.Exp, scale=-1.0)
+
+        def put(lo, hi):
+            for n in range(OUT_TILES):
+                nc.vector.tensor_tensor(res[n][:].indirect(list4[:, cols16(lo, hi)]),
+                                        y[n][:, lo:hi], wgo_sb[:, lo:hi], ALU.mult)
+
+        regroup(0)
+        last = keep.tile([P, 2 * HALF], F32, name="last", tag="words0", align_bytes=64)
+        rest = [(t, HALF, PL, last[:, (t - 2) * HALF:(t - 1) * HALF]) for t in range(2, ROW_TILES)]
+        for job in rest:
+            pick(*job)
+        for job in second:
+            apply_gain(*job)
+        features(0)
+        regroup(1)
+        for job in upper + rest:
+            apply_gain(*job)
+        put(0, UNIT)
+        regroup(2)
+        regroup(3)
+        for u in range(1, 4):
+            features(u)
+        put(UNIT, HALF)
+        put(HALF, PL)
+        for n in range(OUT_TILES):
+            nc.sync.dma_start(out=out[n * P:(n + 1) * P, :], in_=res[n][:])

@@ -43,17 +43,17 @@ def tile_list_module_discharge_page_kernel(
             return psum.tile(shape, dtype, name="bank%d" % b, tag="bank%d" % b)
 
         tab = [keep.tile([P, T], U32, name="tab%d" % a, tag="tab%d" % a, align_bytes=64) for a in range(PASSES)]
-        tab_sc = keep.tile([P, T], U8, align_bytes=64)
+        tab_sc = keep.tile([P, PASSES, T], U8, align_bytes=64)
         w_sc = keep.tile([P, PASSES, H], U8, align_bytes=64)
         v_sc0 = keep.tile([P, S], U8, align_bytes=64)
-        v_sc1 = keep.tile([P, S], U8, align_bytes=64)
         v = [keep.tile([P, S], U32, name="v%d" % a, align_bytes=64) for a in range(PASSES)]
         list1 = keep.tile([P, S // 16], U16)
         list2 = keep.tile([P, S // 16], U16)
         list3 = keep.tile([P, PL // 16], U16)
         list4 = keep.tile([P, PL // 16], U16)
         w1_first = [keep.tile([P, 4, P], F32, name="w1f%d" % a, tag="w1f%d" % a) for a in range(PASSES)]
-        w1_rest = [keep.tile([P, 4, H - P], F32, name="w1r%d" % a) for a in range(PASSES)]
+        w1_second = [keep.tile([P, 4, P], F32, name="w1s%d" % a) for a in range(PASSES)]
+        w1_rest = [keep.tile([P, 4, H - 2 * P], F32, name="w1r%d" % a) for a in range(PASSES)]
         w2_sb = keep.tile([P, PASSES, 2 * H], U8, align_bytes=64)
         w3_first = keep.tile([P, PASSES, P], U32, align_bytes=64)
         w3_rest = keep.tile([P, PASSES, H - P], U32, align_bytes=64)
@@ -66,8 +66,7 @@ def tile_list_module_discharge_page_kernel(
         warm = keep.tile([P, 8], F32)
         warm2 = keep.tile([P, 8], F32)
 
-        nc.vector.memset(tab_sc[:].bitcast(I32), 0)
-        nc.vector.memset(v_sc1[:].bitcast(I32), 0)
+        nc.vector.memset(tab_sc[:].rearrange("p a c -> p (a c)").bitcast(I32), 0)
         nc.vector.memset(w_sc[:].rearrange("p a c -> p (a c)").bitcast(I32), 0)
         nc.vector.memset(warm[:], 0.0)
         nc.scalar.activation(out=warm2[:], in_=warm[:], func=ACT.Exp)
@@ -83,33 +82,30 @@ def tile_list_module_discharge_page_kernel(
         w1_k = w1.rearrange("(a p j) c -> a p j c", a=PASSES, j=4)
         w3_w = w3_words.rearrange("a p c i -> p a (c i)")
 
-        load_tab(0, 0, T)
+        load_tab(0, 0, T // 2)
         for q in range(4):
-            nc.sync.dma_start(out=tab_sc[32 * q:32 * q + 8, :].bitcast(I32),
-                              in_=tab_scales[:, 4 * q:4 * q + 4, :].bitcast(I32))
+            nc.sync.dma_start(out=tab_sc[32 * q:32 * q + 4].bitcast(I32),
+                              in_=tab_scales[:, 4 * q:4 * q + 4, :].rearrange("a r c -> r a c").bitcast(I32))
         nc.sync.dma_start(list1[:], offs)
-        nc.sync.dma_start(out=w1_first[0][:], in_=w1_k[0][:, :, 0:P])
-        load_tab(1, 0, T // 2)
-        nc.sync.dma_start(out=w1_first[1][:], in_=w1_k[1][:, :, 0:P])
-        nc.vector.tensor_copy(v_sc0[:], tab_sc[:].indirect(list1[:]))
+        load_tab(0, T // 2, T)
+        for a in range(PASSES):
+            nc.sync.dma_start(out=w1_first[a][:], in_=w1_k[a][:, :, 0:P])
         for q in range(4):
-            nc.sync.dma_start(out=v_sc1[32 * q:32 * q + 4, :].bitcast(I32),
-                              in_=v_sc0[32 * q + 4:32 * q + 8, :].bitcast(I32))
-        for q in range(2):
             load_weight_scales(w2_scales, 0, q)
-        load_tab(1, T // 2, T)
+        load_tab(1, 0, T // 2)
         nc.sync.dma_start(out=w2_sb[:].bitcast(I32), in_=w2_words.rearrange("a p c -> p a c").bitcast(I32))
-        for q in range(2, 4):
-            load_weight_scales(w2_scales, 0, q)
+        nc.sync.dma_start(out=w3_first[:].bitcast(I32), in_=w3_w[:, :, 0:4 * P].bitcast(I32))
         for q in range(4):
             load_weight_scales(w3_scales, 4, q)
-        nc.sync.dma_start(out=w3_first[:].bitcast(I32), in_=w3_w[:, :, 0:4 * P].bitcast(I32))
+        load_tab(1, T // 2, T)
         nc.sync.dma_start(out=wgs_sb[:], in_=wgs)
+        for a in range(PASSES):
+            nc.sync.dma_start(out=w1_second[a][:], in_=w1_k[a][:, :, P:2 * P])
         nc.sync.dma_start(list2[:], offs2)
         nc.sync.dma_start(out=page[0][:], in_=page0[0:P, :])
-        for a in range(PASSES):
-            nc.sync.dma_start(out=w1_rest[a][:], in_=w1_k[a][:, :, P:H])
         nc.sync.dma_start(out=w3_rest[:].bitcast(I32), in_=w3_w[:, :, 4 * P:4 * H].bitcast(I32))
+        for a in range(PASSES):
+            nc.sync.dma_start(out=w1_rest[a][:], in_=w1_k[a][:, :, 2 * P:H])
         nc.sync.dma_start(list3[:], offs3)
         with nc.allow_non_contiguous_dma(reason="one gain a partition"):
             nc.sync.dma_start(out=gain_sb[:], in_=gain.rearrange("(t p) -> p t", p=P))
@@ -121,7 +117,7 @@ def tile_list_module_discharge_page_kernel(
         for n in range(OUT_TILES):
             nc.sync.dma_start(out=res[n][:], in_=page1[n * P:(n + 1) * P, :])
 
-        v_sc = [v_sc0, v_sc1]
+        nc.vector.tensor_copy(v_sc0[:], tab_sc[:, 0, :].indirect(list1[:]))
         nc.vector.tensor_copy(v[0][:], tab[0][:].indirect(list1[:]))
 
         def interleave(dst, src):
@@ -129,17 +125,23 @@ def tile_list_module_discharge_page_kernel(
                            in_=src.rearrange("p j (c i) -> p c j i", i=4))
 
         def quantise_w1(t):
-            grouped = ring.tile([P, PASSES, P, 4], BF16, name="w1g", align_bytes=64)
+            if t == 0:
+                grouped = keep.tile([P, PASSES, P, 4], BF16, name="w1g0", tag="w1g0", align_bytes=64)
+            else:
+                grouped = ring.tile([P, PASSES, P, 4], BF16, name="w1g", align_bytes=64)
             for a in range(PASSES):
-                src = w1_first[a][:] if t == 0 else w1_rest[a][:, :, (t - 1) * P:t * P]
+                src = (w1_first, w1_second)[t][a][:] if t < 2 else w1_rest[a][:, :, (t - 2) * P:(t - 1) * P]
                 interleave(grouped[:, a], src)
             codes = keep.tile([P, PASSES * P], U32, name="w1q%d" % t, align_bytes=64)
-            scales = keep.tile([P, PASSES * P], U8, name="w1s%d" % t, align_bytes=64)
+            scales = keep.tile([P, PASSES * P], U8, name="w1sc%d" % t, align_bytes=64)
             nc.vector.quantize_mx(out=codes[:].bitcast(FP8X4), scales=scales[:],
                                   in_=grouped[:].rearrange("p a c j -> p (a c j)"))
             return codes, scales
 
         w1q = [quantise_w1(0)]
+        v_sc1 = keep.tile([P, S], U8, tag="w1g0", align_bytes=64)
+        nc.vector.tensor_copy(v_sc1[:], tab_sc[:, 1, :].indirect(list1[:]))
+        v_sc = [v_sc0, v_sc1]
         for c in range(S // HALF):
             nc.vector.tensor_copy(v[1][:, c * HALF:(c + 1) * HALF],
                                   tab[1][:].indirect(list1[:, cols16(c * HALF, (c + 1) * HALF)]))
@@ -148,34 +150,73 @@ def tile_list_module_discharge_page_kernel(
         make_identity(nc, ident_f[:])
         nc.scalar.copy(out=ident_bf[:], in_=ident_f[:])
 
-        def products(t):
+        def mx_pass(t, c, i, a, acc):
             rows = slice(t * P, (t + 1) * P)
-            p2 = keep.tile([P, S], F32, name="p2")
-            p3 = keep.tile([P, S], F32, name="p3")
-            codes, scales = w1q[t]
+            cs = slice(c * HALF, (c + 1) * HALF)
+            if i == 0:
+                codes, scales = w1q[t]
+                w = codes[:, a * P:(a + 1) * P].bitcast(FP8X4)
+                ws = scales[:, a * P:(a + 1) * P]
+            elif i == 1:
+                w = w2_sb[:, a, 2 * t * P:2 * (t + 1) * P].bitcast(FP4X4)
+                ws = w_sc[:, a, rows]
+            else:
+                src = w3_first[:, a, :] if t == 0 else w3_rest[:, a, (t - 1) * P:t * P]
+                w = src.bitcast(FP8X4)
+                ws = w_sc[4:P, a, rows]
+            nc.tensor.matmul_mx(out=acc[:], lhsT=w, lhsT_scale=ws,
+                                rhs=v[a][:, cs].bitcast(FP8X4), rhs_scale=v_sc[a][:, cs],
+                                start=(a == 0), stop=(a == PASSES - 1))
+
+        def tanh_of(acc):
+            d1 = ring.tile([P, HALF], F32, name="d1")
+            nc.scalar.activation(out=d1[:], in_=acc[:], func=ACT.Tanh)
+            return d1
+
+        def sums(t, c):
+            acc = [bank(3 * c + i, [P, HALF], F32) for i in range(3)]
+            for i in range(3):
+                for a in range(PASSES):
+                    mx_pass(t, c, i, a, acc[i])
+            return tanh_of(acc[0]), acc[1], acc[2]
+
+        def first_tile():
+            p2 = keep.tile([P, S], F32, name="p2", tag="turn1")
+            p3 = keep.tile([P, S], F32, name="p3", tag="p3")
+            best = keep.tile([P, S], F32, name="best", tag="turn0")
+            h = keep.tile([P, S], F32, name="h", tag="turn2")
+            acc = [[bank(3 * c + i, [P, HALF], F32) for i in range(3)] for c in range(S // HALF)]
+            for i in range(3):
+                for c in range(S // HALF):
+                    mx_pass(0, c, i, 0, acc[c][i])
             for c in range(S // HALF):
                 cs = slice(c * HALF, (c + 1) * HALF)
-                acc = [bank(3 * c + i, [P, HALF], F32) for i in range(3)]
                 for i in range(3):
-                    for a in range(PASSES):
-                        if i == 0:
-                            w = codes[:, a * P:(a + 1) * P].bitcast(FP8X4)
-                            ws = scales[:, a * P:(a + 1) * P]
-                        elif i == 1:
-                            w = w2_sb[:, a, 2 * t * P:2 * (t + 1) * P].bitcast(FP4X4)
-                            ws = w_sc[:, a, rows]
-                        else:
-                            src = w3_first[:, a, :] if t == 0 else w3_rest[:, a, (t - 1) * P:t * P]
-                            w = src.bitcast(FP8X4)
-                            ws = w_sc[4:P, a, rows]
-                        nc.tensor.matmul_mx(out=acc[i][:], lhsT=w, lhsT_scale=ws,
-                                            rhs=v[a][:, cs].bitcast(FP8X4), rhs_scale=v_sc[a][:, cs],
-                                            start=(a == 0), stop=(a == PASSES - 1))
-                d1 = ring.tile([P, HALF], F32, name="d1")
-                nc.scalar.activation(out=d1[:], in_=acc[0][:], func=ACT.Tanh)
-                nc.vector.tensor_tensor(p2[:, cs], acc[1][:], d1[:], ALU.mult)
-                nc.vector.tensor_tensor(p3[:, cs], acc[2][:], d1[:], ALU.mult)
-            return p2, p3
+                    mx_pass(0, c, i, 1, acc[c][i])
+                d1, d2, d3 = tanh_of(acc[c][0]), acc[c][1], acc[c][2]
+                nc.vector.tensor_tensor(p2[:, cs], d2[:], d1[:], ALU.mult)
+                nc.vector.tensor_tensor(p3[:, cs], d3[:], d1[:], ALU.mult)
+                nc.vector.tensor_tensor(best[:, cs], p2[:, cs], p3[:, cs], ALU.max)
+                nc.gpsimd.tensor_tensor(h[:, cs], best[:, cs], wgs_sb[:, cs], ALU.mult)
+            for c in range(S // HALF):
+                nc.vector.tensor_copy(page[0][:].indirect(list2[:, cols16(c * HALF, (c + 1) * HALF)]),
+                                      h[:, c * HALF:(c + 1) * HALF])
+
+        def later_tile(t):
+            g = keep.tile([P, S], F32, name="g", tag="turn%d" % (t % 3))
+            p2 = keep.tile([P, S], F32, name="p2", tag="turn%d" % ((t + 1) % 3))
+            p3 = keep.tile([P, S], F32, name="p3", tag="p3")
+            h = keep.tile([P, S], F32, name="h", tag="turn%d" % ((t + 2) % 3))
+            for c in range(S // HALF):
+                cs = slice(c * HALF, (c + 1) * HALF)
+                d1, d2, d3 = sums(t, c)
+                d3_sb = ring.tile([P, HALF], F32, name="d3_sb")
+                nc.scalar.copy(out=d3_sb[:], in_=d3[:])
+                nc.gpsimd.tensor_tensor(g[:, cs], d1[:], wgs_sb[:, cs], ALU.mult)
+                nc.gpsimd.tensor_tensor(p3[:, cs], d3_sb[:], g[:, cs], ALU.mult)
+                nc.vector.tensor_tensor(p2[:, cs], d2[:], g[:, cs], ALU.mult)
+            nc.vector.tensor_tensor(h[:], p2[:], p3[:], ALU.max)
+            nc.vector.tensor_copy(page[t][:].indirect(list2[:]), h[:])
 
         x_bf = keep.tile([P, ROW_TILES, PL], BF16, align_bytes=64)
 
@@ -195,41 +236,43 @@ def tile_list_module_discharge_page_kernel(
                 nc.vector.quantize_mx(out=w4q[:, lo:hi].bitcast(FP8X4), scales=w4s[:, lo:hi],
                                       in_=grouped[:, lo:hi, :].rearrange("p c j -> p (c j)"))
 
-        ps = products(0)
+        lasttile = ROW_TILES - 1
         for t in range(ROW_TILES):
-            h = keep.tile([P, S], F32, name="h", tag="h")
-            nc.vector.tensor_tensor(h[:], ps[0][:], ps[1][:], ALU.max)
-            if t + 1 < ROW_TILES:
-                w1q.append(quantise_w1(t + 1))
-                ps = products(t + 1)
-            if t == 1:
+            if t == 0:
+                first_tile()
+                for later in range(1, ROW_TILES):
+                    w1q.append(quantise_w1(later))
                 quantise_w4()
-            nc.vector.tensor_tensor(page[t][:].indirect(list2[:]), h[:], wgs_sb[:], ALU.mult)
-            first = ring.tile([P, UNIT], F32, name="first")
-            pick(t, 0, UNIT, first[:])
-            apply_gain(t, 0, UNIT, first[:])
+            else:
+                later_tile(t)
+            if t < lasttile:
+                early = ring.tile([P, HALF], F32, name="early")
+                pick(t, 0, HALF, early[:])
+                apply_gain(t, 0, HALF, early[:])
 
-        late = keep.tile([P, ROW_TILES * UNIT + 2 * HALF], F32, name="late", tag="h")
-        second = [(t, UNIT, HALF, late[:, t * UNIT:(t + 1) * UNIT]) for t in range(ROW_TILES)]
-        upper = [(t, HALF, PL, late[:, ROW_TILES * UNIT + t * HALF:ROW_TILES * UNIT + (t + 1) * HALF])
-                 for t in range(2)]
-        for job in second + upper:
+        early = ring.tile([P, HALF], F32, name="early")
+        pick(lasttile, 0, UNIT, early[:, 0:UNIT])
+        apply_gain(lasttile, 0, UNIT, early[:, 0:UNIT])
+        pick(lasttile, UNIT, HALF, early[:, UNIT:HALF])
+        late = keep.tile([P, lasttile * HALF], F32, name="late", tag="turn%d" % ((lasttile + 2) % 3))
+        upper = [(t, HALF, PL, late[:, t * HALF:(t + 1) * HALF]) for t in range(lasttile)]
+        for job in upper:
             pick(*job)
 
         xq = keep.tile([P, PL], U32, align_bytes=64)
         xs = keep.tile([P, PL], U8, align_bytes=64)
-        y = [keep.tile([P, PL], F32, name="y%d" % n) for n in range(OUT_TILES)]
+        y = keep.tile([P, OUT_TILES, PL], F32, name="y", tag="y")
 
         def regroup(u):
             us = slice(u * UNIT, (u + 1) * UNIT)
-            turned = bank(6, [P, 2, H], BF16)
+            turned = bank(6 - 2 * (u % 2), [P, 2, H], BF16)
             for b in range(2):
                 lo = u * UNIT + b * P
                 for t in range(ROW_TILES):
                     nc.tensor.transpose(turned[:, b, t * P:(t + 1) * P], x_bf[:, t, lo:lo + P], ident_bf[:])
             pairs = ring.tile([P, 2, 2, P], F32, name="pairs")
             nc.scalar.copy(out=pairs[:], in_=turned[:].bitcast(F32).rearrange("p b (m e) -> p b e m", e=2))
-            back = bank(7, [P, 2, 2, P], F32)
+            back = bank(7 - 2 * (u % 2), [P, 2, 2, P], F32)
             for b in range(2):
                 for e in range(2):
                     nc.tensor.transpose(back[:, b, e, :], pairs[:, b, e, :], ident_f[:])
@@ -238,38 +281,37 @@ def tile_list_module_discharge_page_kernel(
             nc.vector.quantize_mx(out=xq[:, us].bitcast(FP8X4), scales=xs[:, us],
                                   in_=words[:].rearrange("p b c e -> p (b c e)").bitcast(BF16))
 
-        def features(u):
-            us = slice(u * UNIT, (u + 1) * UNIT)
-            for n in range(OUT_TILES):
-                e_acc = bank(3 * (u % 2) + n, [P, UNIT], F32)
-                nc.tensor.matmul_mx(out=e_acc[:], lhsT=w4q[:, n * P:(n + 1) * P].bitcast(FP8X4),
-                                    lhsT_scale=w4s[:, n * P:(n + 1) * P],
-                                    rhs=xq[:, us].bitcast(FP8X4), rhs_scale=xs[:, us], start=True, stop=True)
-                sq = ring.tile([P, UNIT], F32, name="sq")
+        def features(lo, hi, groups, banks):
+            for i, group in enumerate(groups):
+                e_acc = bank(banks[i], [P, len(group), hi - lo], F32)
+                for j, n in enumerate(group):
+                    nc.tensor.matmul_mx(out=e_acc[:, j, :], lhsT=w4q[:, n * P:(n + 1) * P].bitcast(FP8X4),
+                                        lhsT_scale=w4s[:, n * P:(n + 1) * P],
+                                        rhs=xq[:, lo:hi].bitcast(FP8X4), rhs_scale=xs[:, lo:hi],
+                                        start=True, stop=True)
+                sq = ring.tile([P, len(group), hi - lo], F32, name="sq")
                 nc.scalar.activation(out=sq[:], in_=e_acc[:], func=ACT.Square)
-                nc.scalar.activation(out=y[n][:, us], in_=sq[:], func=ACT.Exp, scale=-1.0)
+                nc.scalar.activation(out=y[:, group[0]:group[-1] + 1, lo:hi], in_=sq[:], func=ACT.Exp, scale=-1.0)
 
         def put(lo, hi):
             for n in range(OUT_TILES):
                 nc.vector.tensor_tensor(res[n][:].indirect(list4[:, cols16(lo, hi)]),
-                                        y[n][:, lo:hi], wgo_sb[:, lo:hi], ALU.mult)
+                                        y[:, n, lo:hi], wgo_sb[:, lo:hi], ALU.mult)
 
         regroup(0)
-        last = keep.tile([P, 2 * HALF], F32, name="last", tag="words0", align_bytes=64)
-        rest = [(t, HALF, PL, last[:, (t - 2) * HALF:(t - 1) * HALF]) for t in range(2, ROW_TILES)]
-        for job in rest:
-            pick(*job)
-        for job in second:
-            apply_gain(*job)
-        features(0)
+        last = keep.tile([P, HALF], F32, name="last", tag="words0", align_bytes=64)
+        pick(lasttile, HALF, PL, last[:])
+        apply_gain(lasttile, UNIT, HALF, early[:, UNIT:HALF])
+        features(0, UNIT, ((0,), (1, 2)), (0, 1))
         regroup(1)
-        for job in upper + rest:
+        for job in upper:
             apply_gain(*job)
+        apply_gain(lasttile, HALF, PL, last[:])
         put(0, UNIT)
         regroup(2)
         regroup(3)
-        for u in range(1, 4):
-            features(u)
+        features(UNIT, HALF, ((0,), (1, 2)), (5, 4))
+        features(HALF, PL, ((0,), (1,), (2,)), (0, 1, 2))
         put(UNIT, HALF)
         put(HALF, PL)
         for n in range(OUT_TILES):

@@ -107,10 +107,11 @@ def tile_list_module_discharge_page_kernel(
         for a in range(PASSES):
             nc.sync.dma_start(out=w1_rest[a][:], in_=w1_k[a][:, :, 2 * P:H])
         nc.sync.dma_start(list3[:], offs3)
+        nc.sync.dma_start(out=page[1][:], in_=page0[P:2 * P, :])
         with nc.allow_non_contiguous_dma(reason="one gain a partition"):
             nc.sync.dma_start(out=gain_sb[:], in_=gain.rearrange("(t p) -> p t", p=P))
         nc.sync.dma_start(out=w4_raw[:], in_=w4.rearrange("(p j) n -> p j n", j=4))
-        for t in range(1, ROW_TILES):
+        for t in range(2, ROW_TILES):
             nc.sync.dma_start(out=page[t][:], in_=page0[t * P:(t + 1) * P, :])
         nc.sync.dma_start(list4[:], offs4)
         nc.sync.dma_start(out=wgo_sb[:], in_=wgo)
@@ -125,10 +126,7 @@ def tile_list_module_discharge_page_kernel(
                            in_=src.rearrange("p j (c i) -> p c j i", i=4))
 
         def quantise_w1(t):
-            if t == 0:
-                grouped = keep.tile([P, PASSES, P, 4], BF16, name="w1g0", tag="w1g0", align_bytes=64)
-            else:
-                grouped = ring.tile([P, PASSES, P, 4], BF16, name="w1g", align_bytes=64)
+            grouped = keep.tile([P, PASSES, P, 4], BF16, name="w1g", tag="w1g%d" % t, align_bytes=64)
             for a in range(PASSES):
                 src = (w1_first, w1_second)[t][a][:] if t < 2 else w1_rest[a][:, :, (t - 2) * P:(t - 1) * P]
                 interleave(grouped[:, a], src)
@@ -145,8 +143,8 @@ def tile_list_module_discharge_page_kernel(
         for c in range(S // HALF):
             nc.vector.tensor_copy(v[1][:, c * HALF:(c + 1) * HALF],
                                   tab[1][:].indirect(list1[:, cols16(c * HALF, (c + 1) * HALF)]))
-        ident_f = keep.tile([P, P], F32, tag="tab1", align_bytes=64)
-        ident_bf = keep.tile([P, P], BF16, tag="tab0", align_bytes=64)
+        ident_f = keep.tile([P, P], F32)
+        ident_bf = keep.tile([P, P], BF16)
         make_identity(nc, ident_f[:])
         nc.scalar.copy(out=ident_bf[:], in_=ident_f[:])
 
@@ -182,7 +180,7 @@ def tile_list_module_discharge_page_kernel(
 
         def first_tile():
             p2 = keep.tile([P, S], F32, name="p2", tag="turn1")
-            p3 = keep.tile([P, S], F32, name="p3", tag="p3")
+            p3 = keep.tile([P, S], F32, name="p3", tag="p3", align_bytes=64)
             best = keep.tile([P, S], F32, name="best", tag="turn0")
             h = keep.tile([P, S], F32, name="h", tag="turn2")
             acc = [[bank(3 * c + i, [P, HALF], F32) for i in range(3)] for c in range(S // HALF)]
@@ -205,7 +203,7 @@ def tile_list_module_discharge_page_kernel(
         def later_tile(t):
             g = keep.tile([P, S], F32, name="g", tag="turn%d" % (t % 3))
             p2 = keep.tile([P, S], F32, name="p2", tag="turn%d" % ((t + 1) % 3))
-            p3 = keep.tile([P, S], F32, name="p3", tag="p3")
+            p3 = keep.tile([P, S], F32, name="p3", tag="p3", align_bytes=64)
             h = keep.tile([P, S], F32, name="h", tag="turn%d" % ((t + 2) % 3))
             for c in range(S // HALF):
                 cs = slice(c * HALF, (c + 1) * HALF)
@@ -226,15 +224,17 @@ def tile_list_module_discharge_page_kernel(
         def apply_gain(t, lo, hi, dense):
             nc.scalar.activation(out=x_bf[:, t, lo:hi], in_=dense, func=ACT.Copy, scale=gain_sb[:, t:t + 1])
 
-        w4q = keep.tile([P, N], U32, align_bytes=64)
         w4s = keep.tile([P, N], U8, align_bytes=64)
 
+        w4g = keep.tile([P, N, 4], BF16, name="w4g", align_bytes=64)
+
         def quantise_w4():
-            grouped = keep.tile([P, N, 4], BF16, name="w4g", align_bytes=64)
-            interleave(grouped[:], w4_raw[:])
+            grouped = w4g
+            w4q = keep.tile([P, N], U32, tag="p3", align_bytes=64)
             for lo, hi in ((0, 256), (256, N)):
                 nc.vector.quantize_mx(out=w4q[:, lo:hi].bitcast(FP8X4), scales=w4s[:, lo:hi],
                                       in_=grouped[:, lo:hi, :].rearrange("p c j -> p (c j)"))
+            return w4q
 
         lasttile = ROW_TILES - 1
         for t in range(ROW_TILES):
@@ -242,14 +242,15 @@ def tile_list_module_discharge_page_kernel(
                 first_tile()
                 for later in range(1, ROW_TILES):
                     w1q.append(quantise_w1(later))
-                quantise_w4()
+                interleave(w4g[:], w4_raw[:])
             else:
                 later_tile(t)
             if t < lasttile:
-                early = ring.tile([P, HALF], F32, name="early")
+                early = keep.tile([P, HALF], F32, name="early", tag="w1g%d" % (lasttile - t), align_bytes=64)
                 pick(t, 0, HALF, early[:])
                 apply_gain(t, 0, HALF, early[:])
 
+        w4q = quantise_w4()
         early = ring.tile([P, HALF], F32, name="early")
         pick(lasttile, 0, UNIT, early[:, 0:UNIT])
         apply_gain(lasttile, 0, UNIT, early[:, 0:UNIT])

@@ -125,19 +125,21 @@ def tile_list_module_discharge_page_kernel(
             nc.scalar.copy(out=dst.rearrange("p (c i) j -> p c j i", i=4),
                            in_=src.rearrange("p j (c i) -> p c j i", i=4))
 
-        def quantise_w1(t):
-            grouped = keep.tile([P, PASSES, P, 4], BF16, name="w1g", tag="w1g%d" % t, align_bytes=64)
-            for a in range(PASSES):
+        w1q = {}
+
+        def quantise_w1(jobs, tag):
+            grouped = keep.tile([P, len(jobs), P, 4], BF16, name="w1g", tag=tag, align_bytes=64)
+            codes = keep.tile([P, len(jobs) * P], U32, name="q_" + tag, align_bytes=64)
+            scales = keep.tile([P, len(jobs) * P], U8, name="s_" + tag, align_bytes=64)
+            for i, (t, a) in enumerate(jobs):
                 src = (w1_first, w1_second)[t][a][:] if t < 2 else w1_rest[a][:, :, (t - 2) * P:(t - 1) * P]
-                interleave(grouped[:, a], src)
-            codes = keep.tile([P, PASSES * P], U32, name="w1q%d" % t, align_bytes=64)
-            scales = keep.tile([P, PASSES * P], U8, name="w1sc%d" % t, align_bytes=64)
+                interleave(grouped[:, i], src)
+                w1q[(t, a)] = (codes[:, i * P:(i + 1) * P], scales[:, i * P:(i + 1) * P])
             nc.vector.quantize_mx(out=codes[:].bitcast(FP8X4), scales=scales[:],
                                   in_=grouped[:].rearrange("p a c j -> p (a c j)"))
-            return codes, scales
 
-        w1q = [quantise_w1(0)]
-        v_sc1 = keep.tile([P, S], U8, tag="w1g0", align_bytes=64)
+        quantise_w1([(0, 0), (0, 1)], "w1g00")
+        v_sc1 = keep.tile([P, S], U8, tag="w1g00", align_bytes=64)
         nc.vector.tensor_copy(v_sc1[:], tab_sc[:, 1, :].indirect(list1[:]))
         v_sc = [v_sc0, v_sc1]
         for c in range(S // HALF):
@@ -152,9 +154,8 @@ def tile_list_module_discharge_page_kernel(
             rows = slice(t * P, (t + 1) * P)
             cs = slice(c * HALF, (c + 1) * HALF)
             if i == 0:
-                codes, scales = w1q[t]
-                w = codes[:, a * P:(a + 1) * P].bitcast(FP8X4)
-                ws = scales[:, a * P:(a + 1) * P]
+                codes, ws = w1q[(t, a)]
+                w = codes.bitcast(FP8X4)
             elif i == 1:
                 w = w2_sb[:, a, 2 * t * P:2 * (t + 1) * P].bitcast(FP4X4)
                 ws = w_sc[:, a, rows]
@@ -166,23 +167,12 @@ def tile_list_module_discharge_page_kernel(
                                 rhs=v[a][:, cs].bitcast(FP8X4), rhs_scale=v_sc[a][:, cs],
                                 start=(a == 0), stop=(a == PASSES - 1))
 
-        def tanh_of(acc):
-            d1 = ring.tile([P, HALF], F32, name="d1")
-            nc.scalar.activation(out=d1[:], in_=acc[:], func=ACT.Tanh)
-            return d1
-
-        def sums(t, c):
-            acc = [bank(3 * c + i, [P, HALF], F32) for i in range(3)]
-            for i in range(3):
-                for a in range(PASSES):
-                    mx_pass(t, c, i, a, acc[i])
-            return tanh_of(acc[0]), acc[1], acc[2]
-
         def first_tile():
-            p2 = keep.tile([P, S], F32, name="p2", tag="turn1")
+            d1 = keep.tile([P, S], F32, name="d1", tag="d1")
+            p2 = keep.tile([P, S], F32, name="p2", tag="swap1")
             p3 = keep.tile([P, S], F32, name="p3", tag="p3", align_bytes=64)
-            best = keep.tile([P, S], F32, name="best", tag="turn0")
-            h = keep.tile([P, S], F32, name="h", tag="turn2")
+            best = keep.tile([P, S], F32, name="best", tag="swap0")
+            h = keep.tile([P, S], F32, name="h", tag="h")
             acc = [[bank(3 * c + i, [P, HALF], F32) for i in range(3)] for c in range(S // HALF)]
             for i in range(3):
                 for c in range(S // HALF):
@@ -191,9 +181,9 @@ def tile_list_module_discharge_page_kernel(
                 cs = slice(c * HALF, (c + 1) * HALF)
                 for i in range(3):
                     mx_pass(0, c, i, 1, acc[c][i])
-                d1, d2, d3 = tanh_of(acc[c][0]), acc[c][1], acc[c][2]
-                nc.vector.tensor_tensor(p2[:, cs], d2[:], d1[:], ALU.mult)
-                nc.vector.tensor_tensor(p3[:, cs], d3[:], d1[:], ALU.mult)
+                nc.scalar.activation(out=d1[:, cs], in_=acc[c][0][:], func=ACT.Tanh)
+                nc.vector.tensor_tensor(p2[:, cs], acc[c][1][:], d1[:, cs], ALU.mult)
+                nc.vector.tensor_tensor(p3[:, cs], acc[c][2][:], d1[:, cs], ALU.mult)
                 nc.vector.tensor_tensor(best[:, cs], p2[:, cs], p3[:, cs], ALU.max)
                 nc.gpsimd.tensor_tensor(h[:, cs], best[:, cs], wgs_sb[:, cs], ALU.mult)
             for c in range(S // HALF):
@@ -201,22 +191,32 @@ def tile_list_module_discharge_page_kernel(
                                       h[:, c * HALF:(c + 1) * HALF])
 
         def later_tile(t):
-            g = keep.tile([P, S], F32, name="g", tag="turn%d" % (t % 3))
-            p2 = keep.tile([P, S], F32, name="p2", tag="turn%d" % ((t + 1) % 3))
+            d1 = keep.tile([P, S], F32, name="d1", tag="d1")
+            d2 = keep.tile([P, S], F32, name="d2", tag="d2")
+            d3 = keep.tile([P, S], F32, name="d3", tag="d3", align_bytes=64)
+            g = keep.tile([P, S], F32, name="g", tag="swap%d" % (t % 2))
+            p2 = keep.tile([P, S], F32, name="p2", tag="swap%d" % ((t + 1) % 2))
             p3 = keep.tile([P, S], F32, name="p3", tag="p3", align_bytes=64)
-            h = keep.tile([P, S], F32, name="h", tag="turn%d" % ((t + 2) % 3))
-            for c in range(S // HALF):
-                cs = slice(c * HALF, (c + 1) * HALF)
-                d1, d2, d3 = sums(t, c)
-                d3_sb = ring.tile([P, HALF], F32, name="d3_sb")
-                nc.scalar.copy(out=d3_sb[:], in_=d3[:])
-                nc.gpsimd.tensor_tensor(g[:, cs], d1[:], wgs_sb[:, cs], ALU.mult)
-                nc.gpsimd.tensor_tensor(p3[:, cs], d3_sb[:], g[:, cs], ALU.mult)
-                nc.vector.tensor_tensor(p2[:, cs], d2[:], g[:, cs], ALU.mult)
+            h = keep.tile([P, S], F32, name="h", tag="h")
+            for i in range(3):
+                for c in range(S // HALF):
+                    cs = slice(c * HALF, (c + 1) * HALF)
+                    acc = bank(3 * c + i, [P, HALF], F32)
+                    for a in range(PASSES):
+                        mx_pass(t, c, i, a, acc)
+                    if i == 0:
+                        nc.scalar.activation(out=d1[:, cs], in_=acc[:], func=ACT.Tanh)
+                    else:
+                        nc.scalar.copy(out=(d2, d3)[i - 1][:, cs], in_=acc[:])
+            nc.gpsimd.tensor_tensor(g[:], d1[:], wgs_sb[:], ALU.mult)
+            nc.gpsimd.tensor_tensor(p2[:], d2[:], g[:], ALU.mult)
+            nc.gpsimd.tensor_tensor(p3[:], d3[:], g[:], ALU.mult)
             nc.vector.tensor_tensor(h[:], p2[:], p3[:], ALU.max)
             nc.vector.tensor_copy(page[t][:].indirect(list2[:]), h[:])
 
-        x_bf = keep.tile([P, ROW_TILES, PL], BF16, align_bytes=64)
+        first_tile()
+        quantise_w1([(1, 0), (1, 1)], "w1g1")
+        quantise_w1([(2, 0), (2, 1), (3, 0), (3, 1)], "w1g23")
 
         def pick(t, lo, hi, dense):
             nc.vector.tensor_copy(dense, page[t][:].indirect(list3[:, cols16(lo, hi)]))
@@ -237,32 +237,33 @@ def tile_list_module_discharge_page_kernel(
             return w4q
 
         lasttile = ROW_TILES - 1
+        lower = []
         for t in range(ROW_TILES):
             if t == 0:
-                first_tile()
-                for later in range(1, ROW_TILES):
-                    w1q.append(quantise_w1(later))
                 interleave(w4g[:], w4_raw[:])
             else:
                 later_tile(t)
             if t < lasttile:
-                early = keep.tile([P, HALF], F32, name="early", tag="w1g%d" % (lasttile - t), align_bytes=64)
+                early = keep.tile([P, HALF], F32, name="early%d" % t)
                 pick(t, 0, HALF, early[:])
-                apply_gain(t, 0, HALF, early[:])
+                lower.append((t, 0, HALF, early[:]))
 
+        x_bf = keep.tile([P, ROW_TILES, PL], BF16, tag="d3", align_bytes=64)
+        for job in lower:
+            apply_gain(*job)
         w4q = quantise_w4()
-        early = ring.tile([P, HALF], F32, name="early")
+        early = keep.tile([P, HALF], F32, name="early3")
         pick(lasttile, 0, UNIT, early[:, 0:UNIT])
         apply_gain(lasttile, 0, UNIT, early[:, 0:UNIT])
         pick(lasttile, UNIT, HALF, early[:, UNIT:HALF])
-        late = keep.tile([P, lasttile * HALF], F32, name="late", tag="turn%d" % ((lasttile + 2) % 3))
+        late = keep.tile([P, lasttile * HALF], F32, name="late", tag="h")
         upper = [(t, HALF, PL, late[:, t * HALF:(t + 1) * HALF]) for t in range(lasttile)]
         for job in upper:
             pick(*job)
 
         xq = keep.tile([P, PL], U32, align_bytes=64)
         xs = keep.tile([P, PL], U8, align_bytes=64)
-        y = keep.tile([P, OUT_TILES, PL], F32, name="y", tag="y")
+        y = keep.tile([P, OUT_TILES, PL], F32, name="y", tag="tab0", align_bytes=64)
 
         def regroup(u):
             us = slice(u * UNIT, (u + 1) * UNIT)

@@ -18,14 +18,17 @@ ACT = mybir.ActivationFunctionType
 ALU = mybir.AluOpType
 
 P = 128
-PASSES = K // 512
+PACK = 4
+PASSES = K // (P * PACK)
 ROW_TILES = H // P
+LAST = ROW_TILES - 1
 OUT_TILES = N // P
 HALF = 512
 UNIT = 256
+W3_ROW = 4
 
 
-def cols16(lo, hi):
+def entries(lo, hi):
     return slice(lo // 16, hi // 16)
 
 
@@ -51,9 +54,9 @@ def tile_list_module_discharge_page_kernel(
         list2 = keep.tile([P, S // 16], U16)
         list3 = keep.tile([P, PL // 16], U16)
         list4 = keep.tile([P, PL // 16], U16)
-        w1_first = [keep.tile([P, 4, P], F32, name="w1f%d" % a, tag="w1f%d" % a) for a in range(PASSES)]
-        w1_second = [keep.tile([P, 4, P], F32, name="w1s%d" % a) for a in range(PASSES)]
-        w1_rest = [keep.tile([P, 4, H - 2 * P], F32, name="w1r%d" % a) for a in range(PASSES)]
+        w1_first = [keep.tile([P, PACK, P], F32, name="w1f%d" % a, tag="w1f%d" % a) for a in range(PASSES)]
+        w1_second = [keep.tile([P, PACK, P], F32, name="w1s%d" % a) for a in range(PASSES)]
+        w1_rest = [keep.tile([P, PACK, H - 2 * P], F32, name="w1r%d" % a) for a in range(PASSES)]
         w2_sb = keep.tile([P, PASSES, 2 * H], U8, align_bytes=64)
         w3_first = keep.tile([P, PASSES, P], U32, align_bytes=64)
         w3_rest = keep.tile([P, PASSES, H - P], U32, align_bytes=64)
@@ -61,56 +64,49 @@ def tile_list_module_discharge_page_kernel(
         wgo_sb = keep.tile([P, PL], F32)
         page = [keep.tile([P, T2], F32, name="page%d" % t, align_bytes=64) for t in range(ROW_TILES)]
         res = [keep.tile([P, T2], F32, name="res%d" % n, align_bytes=64) for n in range(OUT_TILES)]
-        w4_raw = keep.tile([P, 4, N], F32)
+        w4_raw = keep.tile([P, PACK, N], F32)
         gain_sb = keep.tile([P, ROW_TILES], F32)
-        warm = keep.tile([P, 8], F32)
-        warm2 = keep.tile([P, 8], F32)
 
         nc.vector.memset(tab_sc[:].rearrange("p a c -> p (a c)").bitcast(I32), 0)
         nc.vector.memset(w_sc[:].rearrange("p a c -> p (a c)").bitcast(I32), 0)
-        nc.vector.memset(warm[:], 0.0)
-        nc.scalar.activation(out=warm2[:], in_=warm[:], func=ACT.Exp)
 
         def load_tab(a, lo, hi):
             nc.sync.dma_start(out=tab[a][:, lo:hi].bitcast(I32),
                               in_=tab_words[a, :, lo:hi, :].rearrange("p t i -> p (t i)").bitcast(I32))
 
-        def load_weight_scales(src, row, q):
-            nc.sync.dma_start(out=w_sc[32 * q + row:32 * q + row + 4].bitcast(I32),
-                              in_=src[:, 4 * q:4 * q + 4, :].rearrange("a r c -> r a c").bitcast(I32))
+        def load_scales(dst, src, first_row):
+            for s in range(PACK):
+                nc.sync.dma_start(out=dst[first_row + s:P:32].bitcast(I32),
+                                  in_=src[:, s:16:PACK, :].rearrange("a q c -> q a c").bitcast(I32))
 
-        w1_k = w1.rearrange("(a p j) c -> a p j c", a=PASSES, j=4)
+        w1_k = w1.rearrange("(a p j) c -> a p j c", a=PASSES, j=PACK)
         w3_w = w3_words.rearrange("a p c i -> p a (c i)")
 
         load_tab(0, 0, T // 2)
-        for q in range(4):
-            nc.sync.dma_start(out=tab_sc[32 * q:32 * q + 4].bitcast(I32),
-                              in_=tab_scales[:, 4 * q:4 * q + 4, :].rearrange("a r c -> r a c").bitcast(I32))
+        load_scales(tab_sc, tab_scales, 0)
         nc.sync.dma_start(list1[:], offs)
         load_tab(0, T // 2, T)
         for a in range(PASSES):
             nc.sync.dma_start(out=w1_first[a][:], in_=w1_k[a][:, :, 0:P])
-        for q in range(4):
-            load_weight_scales(w2_scales, 0, q)
+        load_scales(w_sc, w2_scales, 0)
         load_tab(1, 0, T // 2)
         nc.sync.dma_start(out=w2_sb[:].bitcast(I32), in_=w2_words.rearrange("a p c -> p a c").bitcast(I32))
-        nc.sync.dma_start(out=w3_first[:].bitcast(I32), in_=w3_w[:, :, 0:4 * P].bitcast(I32))
-        for q in range(4):
-            load_weight_scales(w3_scales, 4, q)
+        nc.sync.dma_start(out=w3_first[:].bitcast(I32), in_=w3_w[:, :, 0:PACK * P].bitcast(I32))
+        load_scales(w_sc, w3_scales, W3_ROW)
         load_tab(1, T // 2, T)
         nc.sync.dma_start(out=wgs_sb[:], in_=wgs)
         for a in range(PASSES):
             nc.sync.dma_start(out=w1_second[a][:], in_=w1_k[a][:, :, P:2 * P])
         nc.sync.dma_start(list2[:], offs2)
         nc.sync.dma_start(out=page[0][:], in_=page0[0:P, :])
-        nc.sync.dma_start(out=w3_rest[:].bitcast(I32), in_=w3_w[:, :, 4 * P:4 * H].bitcast(I32))
+        nc.sync.dma_start(out=w3_rest[:].bitcast(I32), in_=w3_w[:, :, PACK * P:PACK * H].bitcast(I32))
         for a in range(PASSES):
             nc.sync.dma_start(out=w1_rest[a][:], in_=w1_k[a][:, :, 2 * P:H])
         nc.sync.dma_start(list3[:], offs3)
         nc.sync.dma_start(out=page[1][:], in_=page0[P:2 * P, :])
         with nc.allow_non_contiguous_dma(reason="one gain a partition"):
             nc.sync.dma_start(out=gain_sb[:], in_=gain.rearrange("(t p) -> p t", p=P))
-        nc.sync.dma_start(out=w4_raw[:], in_=w4.rearrange("(p j) n -> p j n", j=4))
+        nc.sync.dma_start(out=w4_raw[:], in_=w4.rearrange("(p j) n -> p j n", j=PACK))
         for t in range(2, ROW_TILES):
             nc.sync.dma_start(out=page[t][:], in_=page0[t * P:(t + 1) * P, :])
         nc.sync.dma_start(list4[:], offs4)
@@ -128,7 +124,7 @@ def tile_list_module_discharge_page_kernel(
         w1q = {}
 
         def quantise_w1(jobs, tag):
-            grouped = keep.tile([P, len(jobs), P, 4], BF16, name="w1g", tag=tag, align_bytes=64)
+            grouped = keep.tile([P, len(jobs), P, PACK], BF16, name="w1g", tag=tag, align_bytes=64)
             codes = keep.tile([P, len(jobs) * P], U32, name="q_" + tag, align_bytes=64)
             scales = keep.tile([P, len(jobs) * P], U8, name="s_" + tag, align_bytes=64)
             for i, (t, a) in enumerate(jobs):
@@ -144,7 +140,7 @@ def tile_list_module_discharge_page_kernel(
         v_sc = [v_sc0, v_sc1]
         for c in range(S // HALF):
             nc.vector.tensor_copy(v[1][:, c * HALF:(c + 1) * HALF],
-                                  tab[1][:].indirect(list1[:, cols16(c * HALF, (c + 1) * HALF)]))
+                                  tab[1][:].indirect(list1[:, entries(c * HALF, (c + 1) * HALF)]))
         ident_f = keep.tile([P, P], F32)
         ident_bf = keep.tile([P, P], BF16)
         make_identity(nc, ident_f[:])
@@ -162,7 +158,7 @@ def tile_list_module_discharge_page_kernel(
             else:
                 src = w3_first[:, a, :] if t == 0 else w3_rest[:, a, (t - 1) * P:t * P]
                 w = src.bitcast(FP8X4)
-                ws = w_sc[4:P, a, rows]
+                ws = w_sc[W3_ROW:P, a, rows]
             nc.tensor.matmul_mx(out=acc[:], lhsT=w, lhsT_scale=ws,
                                 rhs=v[a][:, cs].bitcast(FP8X4), rhs_scale=v_sc[a][:, cs],
                                 start=(a == 0), stop=(a == PASSES - 1))
@@ -187,7 +183,7 @@ def tile_list_module_discharge_page_kernel(
                 nc.vector.tensor_tensor(best[:, cs], p2[:, cs], p3[:, cs], ALU.max)
                 nc.gpsimd.tensor_tensor(h[:, cs], best[:, cs], wgs_sb[:, cs], ALU.mult)
             for c in range(S // HALF):
-                nc.vector.tensor_copy(page[0][:].indirect(list2[:, cols16(c * HALF, (c + 1) * HALF)]),
+                nc.vector.tensor_copy(page[0][:].indirect(list2[:, entries(c * HALF, (c + 1) * HALF)]),
                                       h[:, c * HALF:(c + 1) * HALF])
 
         def later_tile(t):
@@ -219,45 +215,36 @@ def tile_list_module_discharge_page_kernel(
         quantise_w1([(2, 0), (2, 1), (3, 0), (3, 1)], "w1g23")
 
         def pick(t, lo, hi, dense):
-            nc.vector.tensor_copy(dense, page[t][:].indirect(list3[:, cols16(lo, hi)]))
+            nc.vector.tensor_copy(dense, page[t][:].indirect(list3[:, entries(lo, hi)]))
 
         def apply_gain(t, lo, hi, dense):
             nc.scalar.activation(out=x_bf[:, t, lo:hi], in_=dense, func=ACT.Copy, scale=gain_sb[:, t:t + 1])
 
         w4s = keep.tile([P, N], U8, align_bytes=64)
+        w4g = keep.tile([P, N, PACK], BF16, name="w4g", align_bytes=64)
+        interleave(w4g[:], w4_raw[:])
 
-        w4g = keep.tile([P, N, 4], BF16, name="w4g", align_bytes=64)
-
-        def quantise_w4():
-            grouped = w4g
-            w4q = keep.tile([P, N], U32, tag="p3", align_bytes=64)
-            for lo, hi in ((0, 256), (256, N)):
-                nc.vector.quantize_mx(out=w4q[:, lo:hi].bitcast(FP8X4), scales=w4s[:, lo:hi],
-                                      in_=grouped[:, lo:hi, :].rearrange("p c j -> p (c j)"))
-            return w4q
-
-        lasttile = ROW_TILES - 1
         lower = []
-        for t in range(ROW_TILES):
-            if t == 0:
-                interleave(w4g[:], w4_raw[:])
-            else:
-                later_tile(t)
-            if t < lasttile:
-                early = keep.tile([P, HALF], F32, name="early%d" % t)
-                pick(t, 0, HALF, early[:])
-                lower.append((t, 0, HALF, early[:]))
+        for t in range(LAST):
+            early = keep.tile([P, HALF], F32, name="early%d" % t)
+            pick(t, 0, HALF, early[:])
+            lower.append((t, 0, HALF, early[:]))
+            later_tile(t + 1)
 
         x_bf = keep.tile([P, ROW_TILES, PL], BF16, tag="d3", align_bytes=64)
         for job in lower:
             apply_gain(*job)
-        w4q = quantise_w4()
-        early = keep.tile([P, HALF], F32, name="early3")
-        pick(lasttile, 0, UNIT, early[:, 0:UNIT])
-        apply_gain(lasttile, 0, UNIT, early[:, 0:UNIT])
-        pick(lasttile, UNIT, HALF, early[:, UNIT:HALF])
-        late = keep.tile([P, lasttile * HALF], F32, name="late", tag="h")
-        upper = [(t, HALF, PL, late[:, t * HALF:(t + 1) * HALF]) for t in range(lasttile)]
+        w4q = keep.tile([P, N], U32, tag="p3", align_bytes=64)
+        for lo, hi in ((0, 2 * P), (2 * P, N)):
+            nc.vector.quantize_mx(out=w4q[:, lo:hi].bitcast(FP8X4), scales=w4s[:, lo:hi],
+                                  in_=w4g[:, lo:hi, :].rearrange("p c j -> p (c j)"))
+
+        early = keep.tile([P, HALF], F32, name="early%d" % LAST)
+        pick(LAST, 0, UNIT, early[:, 0:UNIT])
+        apply_gain(LAST, 0, UNIT, early[:, 0:UNIT])
+        pick(LAST, UNIT, HALF, early[:, UNIT:HALF])
+        late = keep.tile([P, LAST * HALF], F32, name="late", tag="h")
+        upper = [(t, HALF, PL, late[:, t * HALF:(t + 1) * HALF]) for t in range(LAST)]
         for job in upper:
             pick(*job)
 
@@ -267,25 +254,25 @@ def tile_list_module_discharge_page_kernel(
 
         def regroup(u):
             us = slice(u * UNIT, (u + 1) * UNIT)
-            turned = bank(6 - 2 * (u % 2), [P, 2, H], BF16)
-            for b in range(2):
+            turned = bank(6 - 2 * (u % 2), [P, UNIT // P, H], BF16)
+            for b in range(UNIT // P):
                 lo = u * UNIT + b * P
                 for t in range(ROW_TILES):
                     nc.tensor.transpose(turned[:, b, t * P:(t + 1) * P], x_bf[:, t, lo:lo + P], ident_bf[:])
-            pairs = ring.tile([P, 2, 2, P], F32, name="pairs")
+            pairs = ring.tile([P, UNIT // P, 2, P], F32, name="pairs")
             nc.scalar.copy(out=pairs[:], in_=turned[:].bitcast(F32).rearrange("p b (m e) -> p b e m", e=2))
-            back = bank(7 - 2 * (u % 2), [P, 2, 2, P], F32)
-            for b in range(2):
+            back = bank(7 - 2 * (u % 2), [P, UNIT // P, 2, P], F32)
+            for b in range(UNIT // P):
                 for e in range(2):
                     nc.tensor.transpose(back[:, b, e, :], pairs[:, b, e, :], ident_f[:])
-            words = keep.tile([P, 2, P, 2], F32, name="words%d" % u, tag="words%d" % u, align_bytes=64)
+            words = keep.tile([P, UNIT // P, P, 2], F32, name="words%d" % u, tag="words%d" % u, align_bytes=64)
             nc.scalar.copy(out=words[:], in_=back[:].rearrange("p b e c -> p b c e"))
             nc.vector.quantize_mx(out=xq[:, us].bitcast(FP8X4), scales=xs[:, us],
                                   in_=words[:].rearrange("p b c e -> p (b c e)").bitcast(BF16))
 
         def features(lo, hi, groups, banks):
-            for i, group in enumerate(groups):
-                e_acc = bank(banks[i], [P, len(group), hi - lo], F32)
+            for group, b in zip(groups, banks):
+                e_acc = bank(b, [P, len(group), hi - lo], F32)
                 for j, n in enumerate(group):
                     nc.tensor.matmul_mx(out=e_acc[:, j, :], lhsT=w4q[:, n * P:(n + 1) * P].bitcast(FP8X4),
                                         lhsT_scale=w4s[:, n * P:(n + 1) * P],
@@ -297,23 +284,26 @@ def tile_list_module_discharge_page_kernel(
 
         def put(lo, hi):
             for n in range(OUT_TILES):
-                nc.vector.tensor_tensor(res[n][:].indirect(list4[:, cols16(lo, hi)]),
+                nc.vector.tensor_tensor(res[n][:].indirect(list4[:, entries(lo, hi)]),
                                         y[:, n, lo:hi], wgo_sb[:, lo:hi], ALU.mult)
+
+        narrow = ((0,), (1, 2))
+        wide = ((0,), (1,), (2,))
 
         regroup(0)
         last = keep.tile([P, HALF], F32, name="last", tag="words0", align_bytes=64)
-        pick(lasttile, HALF, PL, last[:])
-        apply_gain(lasttile, UNIT, HALF, early[:, UNIT:HALF])
-        features(0, UNIT, ((0,), (1, 2)), (0, 1))
+        pick(LAST, HALF, PL, last[:])
+        apply_gain(LAST, UNIT, HALF, early[:, UNIT:HALF])
+        features(0, UNIT, narrow, (0, 1))
         regroup(1)
         for job in upper:
             apply_gain(*job)
-        apply_gain(lasttile, HALF, PL, last[:])
+        apply_gain(LAST, HALF, PL, last[:])
         put(0, UNIT)
         regroup(2)
         regroup(3)
-        features(UNIT, HALF, ((0,), (1, 2)), (5, 4))
-        features(HALF, PL, ((0,), (1,), (2,)), (0, 1, 2))
+        features(UNIT, HALF, narrow, (5, 4))
+        features(HALF, PL, wide, (0, 1, 2))
         put(UNIT, HALF)
         put(HALF, PL)
         for n in range(OUT_TILES):

from contextlib import ExitStack

import concourse.mybir as mybir
from concourse.masks import make_identity

K, T, S, H, T2, PL, N = 1024, 4096, 1024, 512, 2048, 1024, 384
FLOPS = 3 * 2 * K * H * S + 2 * H * N * PL

F32 = mybir.dt.float32
BF16 = mybir.dt.bfloat16
I32 = mybir.dt.int32
U32 = mybir.dt.uint32
U16 = mybir.dt.uint16
U8 = mybir.dt.uint8
FP8X4 = mybir.dt.float8_e4m3fn_x4
FP4X4 = mybir.dt.float4_e2m1fn_x4
ACT = mybir.ActivationFunctionType
ALU = mybir.AluOpType

P = 128
PACK = 4
PASSES = K // (P * PACK)
ROW_TILES = H // P
LAST = ROW_TILES - 1
OUT_TILES = N // P
HALF = 512
UNIT = 256
W3_ROW = 4


def entries(lo, hi):
    return slice(lo // 16, hi // 16)


def tile_list_module_discharge_page_kernel(
    tc, tab_words, tab_scales, offs, offs2, offs3, offs4, w1, w2_words, w2_scales,
    w3_words, w3_scales, wgs, page0, gain, w4, wgo, page1, out,
):
    nc = tc.nc
    with ExitStack() as ctx:
        keep = ctx.enter_context(tc.tile_pool(name="keep", bufs=1))
        ring = ctx.enter_context(tc.tile_pool(name="ring", bufs=2))
        psum = ctx.enter_context(tc.psum_pool(name="psum", bufs=1))

        def bank(b, shape, dtype):
            return psum.tile(shape, dtype, name="bank%d" % b, tag="bank%d" % b)

        tab = [keep.tile([P, T], U32, name="tab%d" % a, tag="tab%d" % a, align_bytes=64) for a in range(PASSES)]
        tab_sc = keep.tile([P, PASSES, T], U8, align_bytes=64)
        w_sc = keep.tile([P, PASSES, H], U8, align_bytes=64)
        v_sc0 = keep.tile([P, S], U8, align_bytes=64)
        v = [keep.tile([P, S], U32, name="v%d" % a, align_bytes=64) for a in range(PASSES)]
        list1 = keep.tile([P, S // 16], U16)
        list2 = keep.tile([P, S // 16], U16)
        list3 = keep.tile([P, PL // 16], U16)
        list4 = keep.tile([P, PL // 16], U16)
        w1_first = [keep.tile([P, PACK, P], F32, name="w1f%d" % a, tag="w1f%d" % a) for a in range(PASSES)]
        w1_second = [keep.tile([P, PACK, P], F32, name="w1s%d" % a) for a in range(PASSES)]
        w1_rest = [keep.tile([P, PACK, H - 2 * P], F32, name="w1r%d" % a) for a in range(PASSES)]
        w2_sb = keep.tile([P, PASSES, 2 * H], U8, align_bytes=64)
        w3_first = keep.tile([P, PASSES, P], U32, align_bytes=64)
        w3_rest = keep.tile([P, PASSES, H - P], U32, align_bytes=64)
        wgs_sb = keep.tile([P, S], F32)
        wgo_sb = keep.tile([P, PL], F32)
        page = [keep.tile([P, T2], F32, name="page%d" % t, align_bytes=64) for t in range(ROW_TILES)]
        res = [keep.tile([P, T2], F32, name="res%d" % n, align_bytes=64) for n in range(OUT_TILES)]
        w4_raw = keep.tile([P, PACK, N], F32)
        gain_sb = keep.tile([P, ROW_TILES], F32)

        nc.vector.memset(tab_sc[:].rearrange("p a c -> p (a c)").bitcast(I32), 0)
        nc.vector.memset(w_sc[:].rearrange("p a c -> p (a c)").bitcast(I32), 0)

        def load_tab(a, lo, hi):
            nc.sync.dma_start(out=tab[a][:, lo:hi].bitcast(I32),
                              in_=tab_words[a, :, lo:hi, :].rearrange("p t i -> p (t i)").bitcast(I32))

        def load_scales(dst, src, first_row):
            for s in range(PACK):
                nc.sync.dma_start(out=dst[first_row + s:P:32].bitcast(I32),
                                  in_=src[:, s:16:PACK, :].rearrange("a q c -> q a c").bitcast(I32))

        w1_k = w1.rearrange("(a p j) c -> a p j c", a=PASSES, j=PACK)
        w3_w = w3_words.rearrange("a p c i -> p a (c i)")

        load_tab(0, 0, T // 2)
        load_scales(tab_sc, tab_scales, 0)
        nc.sync.dma_start(list1[:], offs)
        load_tab(0, T // 2, T)
        for a in range(PASSES):
            nc.sync.dma_start(out=w1_first[a][:], in_=w1_k[a][:, :, 0:P])
        load_scales(w_sc, w2_scales, 0)
        load_tab(1, 0, T // 2)
        nc.sync.dma_start(out=w2_sb[:].bitcast(I32), in_=w2_words.rearrange("a p c -> p a c").bitcast(I32))
        nc.sync.dma_start(out=w3_first[:].bitcast(I32), in_=w3_w[:, :, 0:PACK * P].bitcast(I32))
        load_scales(w_sc, w3_scales, W3_ROW)
        load_tab(1, T // 2, T)
        nc.sync.dma_start(out=wgs_sb[:], in_=wgs)
        for a in range(PASSES):
            nc.sync.dma_start(out=w1_second[a][:], in_=w1_k[a][:, :, P:2 * P])
        nc.sync.dma_start(list2[:], offs2)
        nc.sync.dma_start(out=page[0][:], in_=page0[0:P, :])
        nc.sync.dma_start(out=w3_rest[:].bitcast(I32), in_=w3_w[:, :, PACK * P:PACK * H].bitcast(I32))
        for a in range(PASSES):
            nc.sync.dma_start(out=w1_rest[a][:], in_=w1_k[a][:, :, 2 * P:H])
        nc.sync.dma_start(list3[:], offs3)
        nc.sync.dma_start(out=page[1][:], in_=page0[P:2 * P, :])
        with nc.allow_non_contiguous_dma(reason="one gain a partition"):
            nc.sync.dma_start(out=gain_sb[:], in_=gain.rearrange("(t p) -> p t", p=P))
        nc.sync.dma_start(out=w4_raw[:], in_=w4.rearrange("(p j) n -> p j n", j=PACK))
        for t in range(2, ROW_TILES):
            nc.sync.dma_start(out=page[t][:], in_=page0[t * P:(t + 1) * P, :])
        nc.sync.dma_start(list4[:], offs4)
        nc.sync.dma_start(out=wgo_sb[:], in_=wgo)
        for n in range(OUT_TILES):
            nc.sync.dma_start(out=res[n][:], in_=page1[n * P:(n + 1) * P, :])

        nc.vector.tensor_copy(v_sc0[:], tab_sc[:, 0, :].indirect(list1[:]))
        nc.vector.tensor_copy(v[0][:], tab[0][:].indirect(list1[:]))

        def interleave(dst, src):
            nc.scalar.copy(out=dst.rearrange("p (c i) j -> p c j i", i=4),
                           in_=src.rearrange("p j (c i) -> p c j i", i=4))

        w1q = {}

        def quantise_w1(jobs, tag):
            grouped = keep.tile([P, len(jobs), P, PACK], BF16, name="w1g", tag=tag, align_bytes=64)
            codes = keep.tile([P, len(jobs) * P], U32, name="q_" + tag, align_bytes=64)
            scales = keep.tile([P, len(jobs) * P], U8, name="s_" + tag, align_bytes=64)
            for i, (t, a) in enumerate(jobs):
                src = (w1_first, w1_second)[t][a][:] if t < 2 else w1_rest[a][:, :, (t - 2) * P:(t - 1) * P]
                interleave(grouped[:, i], src)
                w1q[(t, a)] = (codes[:, i * P:(i + 1) * P], scales[:, i * P:(i + 1) * P])
            nc.vector.quantize_mx(out=codes[:].bitcast(FP8X4), scales=scales[:],
                                  in_=grouped[:].rearrange("p a c j -> p (a c j)"))

        quantise_w1([(0, 0), (0, 1)], "w1g00")
        v_sc1 = keep.tile([P, S], U8, tag="w1g00", align_bytes=64)
        nc.vector.tensor_copy(v_sc1[:], tab_sc[:, 1, :].indirect(list1[:]))
        v_sc = [v_sc0, v_sc1]
        for c in range(S // HALF):
            nc.vector.tensor_copy(v[1][:, c * HALF:(c + 1) * HALF],
                                  tab[1][:].indirect(list1[:, entries(c * HALF, (c + 1) * HALF)]))
        ident_f = keep.tile([P, P], F32)
        ident_bf = keep.tile([P, P], BF16)
        make_identity(nc, ident_f[:])
        nc.scalar.copy(out=ident_bf[:], in_=ident_f[:])

        def mx_pass(t, c, i, a, acc):
            rows = slice(t * P, (t + 1) * P)
            cs = slice(c * HALF, (c + 1) * HALF)
            if i == 0:
                codes, ws = w1q[(t, a)]
                w = codes.bitcast(FP8X4)
            elif i == 1:
                w = w2_sb[:, a, 2 * t * P:2 * (t + 1) * P].bitcast(FP4X4)
                ws = w_sc[:, a, rows]
            else:
                src = w3_first[:, a, :] if t == 0 else w3_rest[:, a, (t - 1) * P:t * P]
                w = src.bitcast(FP8X4)
                ws = w_sc[W3_ROW:P, a, rows]
            nc.tensor.matmul_mx(out=acc[:], lhsT=w, lhsT_scale=ws,
                                rhs=v[a][:, cs].bitcast(FP8X4), rhs_scale=v_sc[a][:, cs],
                                start=(a == 0), stop=(a == PASSES - 1))

        def first_tile():
            d1 = keep.tile([P, S], F32, name="d1", tag="d1")
            p2 = keep.tile([P, S], F32, name="p2", tag="swap1")
            p3 = keep.tile([P, S], F32, name="p3", tag="p3", align_bytes=64)
            best = keep.tile([P, S], F32, name="best", tag="swap0")
            h = keep.tile([P, S], F32, name="h", tag="h")
            acc = [[bank(3 * c + i, [P, HALF], F32) for i in range(3)] for c in range(S // HALF)]
            for i in range(3):
                for c in range(S // HALF):
                    mx_pass(0, c, i, 0, acc[c][i])
            for c in range(S // HALF):
                cs = slice(c * HALF, (c + 1) * HALF)
                for i in range(3):
                    mx_pass(0, c, i, 1, acc[c][i])
                nc.scalar.activation(out=d1[:, cs], in_=acc[c][0][:], func=ACT.Tanh)
                nc.vector.tensor_tensor(p2[:, cs], acc[c][1][:], d1[:, cs], ALU.mult)
                nc.vector.tensor_tensor(p3[:, cs], acc[c][2][:], d1[:, cs], ALU.mult)
                nc.vector.tensor_tensor(best[:, cs], p2[:, cs], p3[:, cs], ALU.max)
                nc.gpsimd.tensor_tensor(h[:, cs], best[:, cs], wgs_sb[:, cs], ALU.mult)
            for c in range(S // HALF):
                nc.vector.tensor_copy(page[0][:].indirect(list2[:, entries(c * HALF, (c + 1) * HALF)]),
                                      h[:, c * HALF:(c + 1) * HALF])

        def later_tile(t):
            d1 = keep.tile([P, S], F32, name="d1", tag="d1")
            d2 = keep.tile([P, S], F32, name="d2", tag="d2")
            d3 = keep.tile([P, S], F32, name="d3", tag="d3", align_bytes=64)
            g = keep.tile([P, S], F32, name="g", tag="swap%d" % (t % 2))
            p2 = keep.tile([P, S], F32, name="p2", tag="swap%d" % ((t + 1) % 2))
            p3 = keep.tile([P, S], F32, name="p3", tag="p3", align_bytes=64)
            h = keep.tile([P, S], F32, name="h", tag="h")
            for i in range(3):
                for c in range(S // HALF):
                    cs = slice(c * HALF, (c + 1) * HALF)
                    acc = bank(3 * c + i, [P, HALF], F32)
                    for a in range(PASSES):
                        mx_pass(t, c, i, a, acc)
                    if i == 0:
                        nc.scalar.activation(out=d1[:, cs], in_=acc[:], func=ACT.Tanh)
                    else:
                        nc.scalar.copy(out=(d2, d3)[i - 1][:, cs], in_=acc[:])
            nc.gpsimd.tensor_tensor(g[:], d1[:], wgs_sb[:], ALU.mult)
            nc.gpsimd.tensor_tensor(p2[:], d2[:], g[:], ALU.mult)
            nc.gpsimd.tensor_tensor(p3[:], d3[:], g[:], ALU.mult)
            nc.vector.tensor_tensor(h[:], p2[:], p3[:], ALU.max)
            nc.vector.tensor_copy(page[t][:].indirect(list2[:]), h[:])

        first_tile()
        quantise_w1([(1, 0), (1, 1)], "w1g1")
        quantise_w1([(2, 0), (2, 1), (3, 0), (3, 1)], "w1g23")

        def pick(t, lo, hi, dense):
            nc.vector.tensor_copy(dense, page[t][:].indirect(list3[:, entries(lo, hi)]))

        def apply_gain(t, lo, hi, dense):
            nc.scalar.activation(out=x_bf[:, t, lo:hi], in_=dense, func=ACT.Copy, scale=gain_sb[:, t:t + 1])

        w4s = keep.tile([P, N], U8, align_bytes=64)
        w4g = keep.tile([P, N, PACK], BF16, name="w4g", align_bytes=64)
        interleave(w4g[:], w4_raw[:])

        lower = []
        for t in range(LAST):
            early = keep.tile([P, HALF], F32, name="early%d" % t)
            pick(t, 0, HALF, early[:])
            lower.append((t, 0, HALF, early[:]))
            later_tile(t + 1)

        x_bf = keep.tile([P, ROW_TILES, PL], BF16, tag="d3", align_bytes=64)
        for job in lower:
            apply_gain(*job)
        w4q = keep.tile([P, N], U32, tag="p3", align_bytes=64)
        for lo, hi in ((0, 2 * P), (2 * P, N)):
            nc.vector.quantize_mx(out=w4q[:, lo:hi].bitcast(FP8X4), scales=w4s[:, lo:hi],
                                  in_=w4g[:, lo:hi, :].rearrange("p c j -> p (c j)"))

        early = keep.tile([P, HALF], F32, name="early%d" % LAST)
        pick(LAST, 0, UNIT, early[:, 0:UNIT])
        apply_gain(LAST, 0, UNIT, early[:, 0:UNIT])
        pick(LAST, UNIT, HALF, early[:, UNIT:HALF])
        late = keep.tile([P, LAST * HALF], F32, name="late", tag="h")
        upper = [(t, HALF, PL, late[:, t * HALF:(t + 1) * HALF]) for t in range(LAST)]
        for job in upper:
            pick(*job)

        xq = keep.tile([P, PL], U32, align_bytes=64)
        xs = keep.tile([P, PL], U8, align_bytes=64)
        y = keep.tile([P, OUT_TILES, PL], F32, name="y", tag="tab0", align_bytes=64)

        def regroup(u):
            us = slice(u * UNIT, (u + 1) * UNIT)
            turned = bank(6 - 2 * (u % 2), [P, UNIT // P, H], BF16)
            for b in range(UNIT // P):
                lo = u * UNIT + b * P
                for t in range(ROW_TILES):
                    nc.tensor.transpose(turned[:, b, t * P:(t + 1) * P], x_bf[:, t, lo:lo + P], ident_bf[:])
            pairs = ring.tile([P, UNIT // P, 2, P], F32, name="pairs")
            nc.scalar.copy(out=pairs[:], in_=turned[:].bitcast(F32).rearrange("p b (m e) -> p b e m", e=2))
            back = bank(7 - 2 * (u % 2), [P, UNIT // P, 2, P], F32)
            for b in range(UNIT // P):
                for e in range(2):
                    nc.tensor.transpose(back[:, b, e, :], pairs[:, b, e, :], ident_f[:])
            words = keep.tile([P, UNIT // P, P, 2], F32, name="words%d" % u, tag="words%d" % u, align_bytes=64)
            nc.scalar.copy(out=words[:], in_=back[:].rearrange("p b e c -> p b c e"))
            nc.vector.quantize_mx(out=xq[:, us].bitcast(FP8X4), scales=xs[:, us],
                                  in_=words[:].rearrange("p b c e -> p (b c e)").bitcast(BF16))

        def features(lo, hi, groups, banks):
            for group, b in zip(groups, banks):
                e_acc = bank(b, [P, len(group), hi - lo], F32)
                for j, n in enumerate(group):
                    nc.tensor.matmul_mx(out=e_acc[:, j, :], lhsT=w4q[:, n * P:(n + 1) * P].bitcast(FP8X4),
                                        lhsT_scale=w4s[:, n * P:(n + 1) * P],
                                        rhs=xq[:, lo:hi].bitcast(FP8X4), rhs_scale=xs[:, lo:hi],
                                        start=True, stop=True)
                sq = ring.tile([P, len(group), hi - lo], F32, name="sq")
                nc.scalar.activation(out=sq[:], in_=e_acc[:], func=ACT.Square)
                nc.scalar.activation(out=y[:, group[0]:group[-1] + 1, lo:hi], in_=sq[:], func=ACT.Exp, scale=-1.0)

        def put(lo, hi):
            for n in range(OUT_TILES):
                nc.vector.tensor_tensor(res[n][:].indirect(list4[:, entries(lo, hi)]),
                                        y[:, n, lo:hi], wgo_sb[:, lo:hi], ALU.mult)

        narrow = ((0,), (1, 2))
        wide = ((0,), (1,), (2,))

        regroup(0)
        last = keep.tile([P, HALF], F32, name="last", tag="words0", align_bytes=64)
        pick(LAST, HALF, PL, last[:])
        apply_gain(LAST, UNIT, HALF, early[:, UNIT:HALF])
        features(0, UNIT, narrow, (0, 1))
        regroup(1)
        for job in upper:
            apply_gain(*job)
        apply_gain(LAST, HALF, PL, last[:])
        put(0, UNIT)
        regroup(2)
        regroup(3)
        features(UNIT, HALF, narrow, (5, 4))
        features(HALF, PL, wide, (0, 1, 2))
        put(UNIT, HALF)
        put(HALF, PL)
        for n in range(OUT_TILES):
            nc.sync.dma_start(out=out[n * P:(n + 1) * P, :], in_=res[n][:])
